import numpy as np
import ml_dtypes


def mxq(x, axis, fmt="e4m3"):
    dtype, down = {"e4m3": (ml_dtypes.float8_e4m3fn, 7), "e5m2": (ml_dtypes.float8_e5m2, 14)}[fmt]
    v = np.moveaxis(np.asarray(x, np.float32).astype(ml_dtypes.bfloat16).astype(np.float64), axis, -1)
    blocks = v.reshape(v.shape[:-1] + (-1, 32))
    amax = np.abs(blocks).max(-1, keepdims=True)
    byte = np.maximum(np.where(amax > 0, np.frexp(amax)[1] - 1 + 127, 0) - down, 1)
    scale = np.exp2(byte - 127.0)
    codes = (blocks / scale).astype(np.float32).astype(dtype).astype(np.float64)
    return np.moveaxis((codes * scale).reshape(v.shape), -1, axis)


WIDE = False


def mx_kscale(k):
    if not WIDE:
        return np.ones(k)
    levels = np.array([10, -10, 5, -5, 0])
    if k % 512:
        return np.exp2(np.random.permutation(np.resize(levels, k // 32))).repeat(32)
    a = np.empty((k // 512, 16))
    for p in range(k // 512):
        a[p, :8] = np.random.permutation(np.resize(levels, 8))
        for g in range(8):
            far = levels[np.abs(levels - a[p, g]) >= 10]
            a[p, g + 8] = far[np.random.randint(len(far))]
    return np.exp2(a.ravel()).repeat(32)


def f64(x):
    return np.asarray(x).astype(np.float64)


def striped(idx):
    return np.tile(idx.reshape(-1, 16).T, (8, 1)).astype(np.uint16)


def unstriped(offs):
    return offs[:16].T.reshape(-1).astype(np.int64)


def striped8(idx):
    return np.concatenate([x.reshape(-1, 16).T for x in idx]).astype(np.uint16)


def runs(offs, k):
    lists = np.stack([offs[16 * r : 16 * r + 16].T.reshape(-1) for r in range(8)]).astype(np.int64)
    return lists[np.arange(k) % 512 // 64]


def pack_weight(w):
    k, n = w.shape
    w = f64(np.asarray(w, np.float32).astype(ml_dtypes.bfloat16)).reshape(k // 32, 32, n)
    amax = np.abs(w).max(1)
    byte = np.clip(np.where(amax > 0, np.frexp(amax)[1] - 1 + 127 - 7, 1), 1, 254)
    scaled = (w * np.exp2(127.0 - byte)[:, None, :]).reshape(k, n).astype(np.float32)
    words = np.ascontiguousarray(scaled.reshape(k // 512, 128, 4, n).transpose(0, 1, 3, 2)).astype(ml_dtypes.float8_e4m3fn).view(np.uint8)
    return words, np.ascontiguousarray(byte.astype(np.uint8).reshape(k // 512, 16, n))


def unpack_weight(words, scales):
    g, p, n, _ = words.shape
    vals = np.ascontiguousarray(words).view(ml_dtypes.float8_e4m3fn).astype(np.float64) * np.repeat(np.exp2(scales.astype(np.float64) - 127.0), 8, axis=1)[..., None]
    return vals.transpose(0, 1, 3, 2).reshape(g * 512, n)

def planes(y):
    n, m = y.shape
    v = y.astype(np.float32).astype(ml_dtypes.bfloat16).astype(np.float64).reshape(n // 32, 32, m)
    top = np.abs(v).max(1)
    byte = np.clip(np.where(top > 0, np.frexp(top)[1] - 1 + 127 - 7, 1), 1, 254)
    codes = (v * np.exp2(127.0 - byte)[:, None, :]).reshape(n, m).astype(np.float32).astype(ml_dtypes.float8_e4m3fn).view(np.uint8)
    words = codes.reshape(n // 512, 128, 4, m).transpose(0, 1, 3, 2)
    return np.ascontiguousarray(words), np.ascontiguousarray(byte.astype(np.uint8).reshape(n // 512, 16, m))


K, T, S, V, H = 512, 2048, 512, 512, 512


def setup_inputs():
    n = np.random.standard_normal
    s = mx_kscale(K)[:, None]
    u = mx_kscale(S)
    packed_xT = pack_weight(n((K, T)) * s)
    packed_w1 = pack_weight(n((K, H)) / np.sqrt(K) / s)
    packed_w2 = pack_weight(n((K, H)) / np.sqrt(K) / s)
    return {
        "x_words": packed_xT[0],
        "x_scales": packed_xT[1],
        "w1_words": packed_w1[0],
        "w1_scales": packed_w1[1],
        "w2_words": packed_w2[0],
        "w2_scales": packed_w2[1],
        "ga": (np.random.uniform(0.5, 1.5, (H, 1)) * u[:, None]).astype(np.float32),
        "gb": (np.random.uniform(0.5, 1.5, (H, 1)) / u[:, None]).astype(np.float32),
        "offs": striped(np.random.permutation(T)[:S]),
        "two": striped(np.random.permutation(T)[:V]),
        "n1": striped8(np.stack([np.random.permutation(S) for _ in range(8)])),
        "c1": striped8(np.stack([np.random.permutation(V) for _ in range(8)])),
        "c2": striped8(np.stack([np.random.permutation(V) for _ in range(8)])),
    }


def reference(x_words, x_scales, w1_words, w1_scales, w2_words, w2_scales, ga, gb, offs, two, n1, c1, c2):
    xq = unpack_weight(x_words, x_scales)[:, unstriped(offs)]
    a = unpack_weight(w1_words, w1_scales).T @ xq
    z = f64(ga) * (a + 0.5 * (a[np.arange(H)[:, None], runs(n1, H)]))
    x_two = unpack_weight(x_words, x_scales)[:, unstriped(two)]
    b = unpack_weight(w2_words, w2_scales).T @ x_two
    z2 = f64(gb) * b
    s = 0.0625 * ((mxq(z, 0, "e4m3").T @ mxq(z2, 0, "e4m3")))
    ex = np.exp(0.5 * s)
    out_0 = ex / (ex + ex[np.arange(S)[:, None], runs(c1, S)] + ex[np.arange(S)[:, None], runs(c2, S)])
    return (out_0,) + planes(out_0)

@@ -1,0 +1,206 @@
+from contextlib import ExitStack
+
+import concourse.mybir as mybir
+
+K, T, S, V, H = 512, 2048, 512, 512, 512
+FLOPS = 3 * 2 * 512 * 512 * 512
+
+F32 = mybir.dt.float32
+BF16 = mybir.dt.bfloat16
+I32 = mybir.dt.int32
+U32 = mybir.dt.uint32
+U16 = mybir.dt.uint16
+U8 = mybir.dt.uint8
+FP8X4 = mybir.dt.float8_e4m3fn_x4
+ACT = mybir.ActivationFunctionType
+ALU = mybir.AluOpType
+
+P = 128
+PACK = 4
+LIST_ROWS = 16
+HALF = 256
+PIECES = (256, 128, 128)
+
+
+def as_words(dram):
+    return dram[0].rearrange("p n t -> p (n t)").bitcast(I32)
+
+
+def entries(lists, first, count):
+    return lists[:, first // LIST_ROWS : (first + count) // LIST_ROWS]
+
+
+def load_scale_rows(queues, plane, rows):
+    for q in range(4):
+        queues[q].dma_start(out=plane[32 * q : 32 * q + 4, :].bitcast(I32), in_=rows[0, 4 * q : 4 * q + 4, :].bitcast(I32))
+
+
+def tile_picked_keylsm_none_po_kernel(
+    tc, x_words, x_scales, w1_words, w1_scales, w2_words, w2_scales, ga, gb, offs, two, n1, c1, c2, out_0, out_1, out_2
+):
+    nc = tc.nc
+    with ExitStack() as ctx:
+        keep = ctx.enter_context(tc.tile_pool(name="keep", bufs=1))
+        psum = ctx.enter_context(tc.psum_pool(name="psum", bufs=1))
+
+        def tile(shape, dtype, name):
+            return keep.tile(shape, dtype, name=name, align_bytes=64)
+
+        offs_t = tile([P, S // LIST_ROWS], U16, "offs_t")
+        two_t = tile([P, V // LIST_ROWS], U16, "two_t")
+        n1_t = tile([P, S // LIST_ROWS], U16, "n1_t")
+        c1_t = tile([P, V // LIST_ROWS], U16, "c1_t")
+        c2_t = tile([P, V // LIST_ROWS], U16, "c2_t")
+        xw = tile([P, T], U32, "xw")
+        xs = tile([P, T], U8, "xs")
+        w_raw = tile([P, H], I32, "w_raw")
+        ws_raw = tile([P, H], U8, "ws_raw")
+        ga_t = tile([P, PACK], F32, "ga_t")
+        gb_t = tile([P, PACK], F32, "gb_t")
+
+        nc.vector.memset(xs[:].bitcast(I32), 0)
+        nc.gpsimd.memset(ws_raw[:].bitcast(I32), 0)
+
+        nc.sync.dma_start(offs_t[:], offs)
+        nc.sync.dma_start(two_t[:], two)
+        load_scale_rows([nc.scalar] * 4, xs, x_scales)
+        nc.sync.dma_start(n1_t[:], n1)
+        nc.sync.dma_start(c1_t[:], c1)
+        nc.sync.dma_start(c2_t[:], c2)
+        nc.sync.dma_start(out=xw[:].bitcast(I32), in_=as_words(x_words))
+        nc.sync.dma_start(out=w_raw[:], in_=as_words(w1_words))
+        load_scale_rows([nc.scalar, nc.scalar, nc.gpsimd, nc.gpsimd], ws_raw, w1_scales)
+        nc.gpsimd.dma_start(out=ga_t[:], in_=ga.rearrange("(p t) o -> p (t o)", t=PACK))
+        nc.gpsimd.dma_start(out=gb_t[:], in_=gb.rearrange("(p t) o -> p (t o)", t=PACK))
+
+        half_ga = tile([P, PACK], F32, "half_ga")
+        nc.scalar.activation(half_ga[:], ga_t[:], ACT.Copy, scale=0.5)
+
+        picked_w = [tile([P, S], U32, f"picked_w{i}") for i in range(2)]
+        picked_s = [tile([P, S], U8, f"picked_s{i}") for i in range(2)]
+        w_dealt = [tile([P, PACK, P], I32, f"w_dealt{i}") for i in range(2)]
+        ws_dealt = [tile([P, PACK, P], U8, f"ws_dealt{i}") for i in range(2)]
+
+        def deal(i):
+            nc.vector.tensor_copy(out=w_dealt[i][:].rearrange("p t m -> p m t"), in_=w_raw[:].rearrange("p (m t) -> p m t", t=PACK))
+            nc.vector.tensor_copy(out=ws_dealt[i][:].rearrange("p t m -> p m t"), in_=ws_raw[:].rearrange("p (m t) -> p m t", t=PACK))
+
+        def project(i):
+            banks = []
+            for t in range(PACK):
+                bank = psum.tile([P, S], F32, name=f"proj{i}{t}", tag=f"bank{i}{t}")
+                nc.tensor.matmul_mx(
+                    out=bank[:],
+                    lhsT=w_dealt[i][:, t, :].bitcast(FP8X4),
+                    lhsT_scale=ws_dealt[i][:, t, :],
+                    rhs=picked_w[i][:].bitcast(FP8X4),
+                    rhs_scale=picked_s[i][:],
+                    start=True,
+                    stop=True,
+                )
+                banks.append(bank)
+            return banks
+
+        nc.vector.tensor_copy(picked_s[0][:], xs[:].indirect(offs_t[:]))
+        nc.vector.tensor_copy(picked_w[0][:], xw[:].indirect(offs_t[:]))
+        deal(0)
+        nc.sync.dma_start(out=w_raw[:], in_=as_words(w2_words))
+        load_scale_rows([nc.sync] * 4, ws_raw, w2_scales)
+        a_banks = project(0)
+        nc.vector.tensor_copy(picked_s[1][:], xs[:].indirect(two_t[:]))
+        nc.vector.tensor_copy(picked_w[1][:], xw[:].indirect(two_t[:]))
+        deal(1)
+        b_banks = project(1)
+
+        z = tile([P, PACK, S], F32, "z")
+        a_full = tile([P, PACK, S], F32, "a_full")
+        for t in range(PACK):
+            a_half = tile([P, S], F32, f"a_half{t}")
+            nc.scalar.activation(a_half[:], a_banks[t][:], ACT.Copy, scale=half_ga[:, t : t + 1])
+            nc.scalar.activation(a_full[:, t, :], a_banks[t][:], ACT.Copy, scale=ga_t[:, t : t + 1])
+            for j in range(0, S, HALF):
+                nc.vector.tensor_tensor(z[:, t, j : j + HALF], a_half[:].indirect(entries(n1_t, j, HALF)), a_full[:, t, j : j + HALF], ALU.add)
+
+        z2 = tile([P, PACK, V], BF16, "z2")
+        for t in range(PACK):
+            nc.scalar.activation(z2[:, t, :], b_banks[t][:], ACT.Copy, scale=gb_t[:, t : t + 1])
+
+        z_grouped = tile([P, S * PACK], BF16, "z_grouped")
+        nc.vector.tensor_copy(
+            out=z_grouped[:].rearrange("p (u m t) -> p m t u", u=PACK, t=PACK), in_=z[:].rearrange("p t (m u) -> p m t u", u=PACK)
+        )
+        z2_grouped = [tile([P, HALF * PACK], BF16, f"z2_grouped{h}") for h in range(2)]
+        for h, copy in enumerate((nc.vector.tensor_copy, nc.scalar.copy)):
+            copy(
+                out=z2_grouped[h][:].rearrange("p (c i t) -> p c t i", i=PACK, t=PACK),
+                in_=z2[:, :, h * HALF : (h + 1) * HALF].rearrange("p t (c i) -> p c t i", i=PACK),
+            )
+        z_codes = tile([P, S], U32, "z_codes")
+        z_scales = tile([P, S], U8, "z_scales")
+        z2_codes = tile([P, V], U32, "z2_codes")
+        z2_scales = tile([P, V], U8, "z2_scales")
+        nc.vector.quantize_mx(out=z_codes[:, :P].bitcast(FP8X4), scales=z_scales[:, :P], in_=z_grouped[:, : P * PACK])
+        for h in range(2):
+            cols = slice(h * HALF, (h + 1) * HALF)
+            nc.vector.quantize_mx(out=z2_codes[:, cols].bitcast(FP8X4), scales=z2_scales[:, cols], in_=z2_grouped[h][:])
+        for u in range(1, PACK):
+            cols = slice(u * P, (u + 1) * P)
+            nc.vector.quantize_mx(out=z_codes[:, cols].bitcast(FP8X4), scales=z_scales[:, cols], in_=z_grouped[:, u * P * PACK : (u + 1) * P * PACK])
+
+        s_banks = []
+        for u in range(PACK):
+            cols = slice(u * P, (u + 1) * P)
+            bank = psum.tile([P, V], F32, name=f"score{u}", tag=f"bank0{u}")
+            nc.tensor.matmul_mx(
+                out=bank[:],
+                lhsT=z_codes[:, cols].bitcast(FP8X4),
+                lhsT_scale=z_scales[:, cols],
+                rhs=z2_codes[:].bitcast(FP8X4),
+                rhs_scale=z2_scales[:],
+                start=True,
+                stop=True,
+            )
+            s_banks.append(bank)
+
+        ex = [tile([P, V], F32, f"ex{u}") for u in range(PACK)]
+        ex_inv = tile([P, PACK, V], F32, "ex_inv")
+        for u in range(PACK):
+            nc.scalar.activation(ex[u][:], s_banks[u][:], ACT.Exp, scale=0.03125)
+        for u in range(PACK):
+            nc.scalar.activation(ex_inv[:, u, :], s_banks[u][:], ACT.Exp, scale=-0.03125)
+
+        out_codes = tile([P, V], U32, "out_codes")
+        out_scales = tile([P, V], U8, "out_scales")
+        out_rows = out_0.rearrange("(p u) v -> p u v", u=PACK)
+        first = 0
+        for k, width in enumerate(PIECES):
+            cols = slice(first, first + width)
+            one = tile([P, PACK, width], F32, f"one{k}")
+            both = tile([P, PACK, width], F32, f"both{k}")
+            ratio = tile([P, PACK, width], F32, f"ratio{k}")
+            root = tile([P, PACK, width], F32, f"root{k}")
+            share = tile([P, PACK, width], F32, f"share{k}")
+            grouped = tile([P, width * PACK], BF16, f"grouped{k}")
+            last = k == len(PIECES) - 1
+            for step in range(PACK + 2):
+                if step < PACK:
+                    u = step
+                    nc.vector.tensor_copy(one[:, u, :], ex[u][:].indirect(entries(c1_t, first, width)))
+                if 1 <= step <= PACK:
+                    u = step - 1
+                    nc.vector.tensor_tensor(both[:, u, :], ex[u][:].indirect(entries(c2_t, first, width)), one[:, u, :], ALU.add)
+                if last and step >= 2:
+                    u = step - 2
+                    nc.vector.tensor_tensor(ratio[:, u, :], both[:, u, :], ex_inv[:, u, cols], ALU.mult)
+                    nc.scalar.activation(root[:, u, :], ratio[:, u, :], ACT.Abs_reciprocal_sqrt, bias=1.0)
+            if not last:
+                nc.vector.tensor_tensor(ratio[:], both[:], ex_inv[:, :, cols], ALU.mult)
+                nc.scalar.activation(root[:], ratio[:], ACT.Abs_reciprocal_sqrt, bias=1.0)
+            nc.scalar.activation(grouped[:].rearrange("p (c u) -> p c u", u=PACK), root[:].rearrange("p u c -> p c u"), ACT.Square)
+            nc.scalar.activation(share[:], root[:], ACT.Square)
+            nc.vector.quantize_mx(out=out_codes[:, cols].bitcast(FP8X4), scales=out_scales[:, cols], in_=grouped[:])
+            nc.sync.dma_start(out=as_words(out_1)[:, cols], in_=out_codes[:, cols].bitcast(I32))
+            nc.sync.dma_start(out=out_rows[:, :, cols], in_=share[:])
+            first = first + width
+        for q in range(4):
+            nc.sync.dma_start(out=out_2[0, 4 * q : 4 * q + 4, :].bitcast(I32), in_=out_scales[32 * q : 32 * q + 4, :].bitcast(I32))

@@ -1,6 +1,7 @@
 from contextlib import ExitStack
 
 import concourse.mybir as mybir
+from concourse.masks import make_identity
 
 K, T, S, V, H = 512, 2048, 512, 512, 512
 FLOPS = 3 * 2 * 512 * 512 * 512
@@ -17,6 +18,7 @@ ALU = mybir.AluOpType
 
 P = 128
 PACK = 4
+RUN = 8
 LIST_ROWS = 16
 HALF = 256
 PIECES = (256, 128, 128)
@@ -30,9 +32,9 @@ def entries(lists, first, count):
     return lists[:, first // LIST_ROWS : (first + count) // LIST_ROWS]
 
 
-def load_scale_rows(queues, plane, rows):
+def load_scale_rows(queue, plane, rows):
     for q in range(4):
-        queues[q].dma_start(out=plane[32 * q : 32 * q + 4, :].bitcast(I32), in_=rows[0, 4 * q : 4 * q + 4, :].bitcast(I32))
+        queue.dma_start(out=plane[32 * q : 32 * q + 4, :].bitcast(I32), in_=rows[0, 4 * q : 4 * q + 4, :].bitcast(I32))
 
 
 def tile_picked_keylsm_none_po_kernel(
@@ -46,6 +48,9 @@ def tile_picked_keylsm_none_po_kernel(
         def tile(shape, dtype, name):
             return keep.tile(shape, dtype, name=name, align_bytes=64)
 
+        def bank(index, name):
+            return psum.tile([P, 512], F32, name=name, tag=f"bank{index}")
+
         offs_t = tile([P, S // LIST_ROWS], U16, "offs_t")
         two_t = tile([P, V // LIST_ROWS], U16, "two_t")
         n1_t = tile([P, S // LIST_ROWS], U16, "n1_t")
@@ -53,62 +58,83 @@ def tile_picked_keylsm_none_po_kernel(
         c2_t = tile([P, V // LIST_ROWS], U16, "c2_t")
         xw = tile([P, T], U32, "xw")
         xs = tile([P, T], U8, "xs")
-        w_raw = tile([P, H], I32, "w_raw")
-        ws_raw = tile([P, H], U8, "ws_raw")
-        ga_t = tile([P, PACK], F32, "ga_t")
-        gb_t = tile([P, PACK], F32, "gb_t")
+        w_raw = [tile([P, H], I32, f"w_raw{i}") for i in range(2)]
+        ws_raw = [tile([P, H], U8, f"ws_raw{i}") for i in range(2)]
+        gain_rows = tile([P, P], F32, "gain_rows")
+        identity = tile([P, P], F32, "identity")
 
         nc.vector.memset(xs[:].bitcast(I32), 0)
-        nc.gpsimd.memset(ws_raw[:].bitcast(I32), 0)
+        nc.vector.memset(ws_raw[0][:].bitcast(I32), 0)
+        nc.gpsimd.memset(gain_rows[:], 0.0)
+
+        def load_gain(gain):
+            nc.gpsimd.dma_start(
+                out=gain_rows[0:PACK, :].rearrange("t (b e) -> t b e", e=RUN), in_=gain.rearrange("(b t e) o -> t b (e o)", t=PACK, e=RUN)
+            )
 
         nc.sync.dma_start(offs_t[:], offs)
         nc.sync.dma_start(two_t[:], two)
-        load_scale_rows([nc.scalar] * 4, xs, x_scales)
         nc.sync.dma_start(n1_t[:], n1)
         nc.sync.dma_start(c1_t[:], c1)
         nc.sync.dma_start(c2_t[:], c2)
         nc.sync.dma_start(out=xw[:].bitcast(I32), in_=as_words(x_words))
-        nc.sync.dma_start(out=w_raw[:], in_=as_words(w1_words))
-        load_scale_rows([nc.scalar, nc.scalar, nc.gpsimd, nc.gpsimd], ws_raw, w1_scales)
-        nc.gpsimd.dma_start(out=ga_t[:], in_=ga.rearrange("(p t) o -> p (t o)", t=PACK))
-        nc.gpsimd.dma_start(out=gb_t[:], in_=gb.rearrange("(p t) o -> p (t o)", t=PACK))
+        load_scale_rows(nc.sync, xs, x_scales)
+        load_scale_rows(nc.sync, ws_raw[0], w1_scales)
+        load_gain(ga)
+        make_identity(nc, identity[:])
+        nc.gpsimd.dma_start(out=w_raw[0][:], in_=as_words(w1_words))
+        nc.gpsimd.memset(ws_raw[1][:].bitcast(I32), 0)
+        nc.gpsimd.dma_start(out=w_raw[1][:], in_=as_words(w2_words))
+        load_scale_rows(nc.sync, ws_raw[1], w2_scales)
 
+        ga_t = tile([P, PACK], F32, "ga_t")
         half_ga = tile([P, PACK], F32, "half_ga")
-        nc.scalar.activation(half_ga[:], ga_t[:], ACT.Copy, scale=0.5)
+        gb_t = tile([P, PACK], F32, "gb_t")
+        turned = bank(6, "ga_turned")
+        nc.tensor.transpose(turned[:, :P], gain_rows[:], identity[:])
+        nc.scalar.activation(half_ga[:], turned[:, :PACK], ACT.Copy, scale=0.5)
+        nc.scalar.copy(ga_t[:], turned[:, :PACK])
+        load_gain(gb)
+        turned = bank(7, "gb_turned")
+        nc.tensor.transpose(turned[:, :P], gain_rows[:], identity[:])
+        nc.scalar.copy(gb_t[:], turned[:, :PACK])
 
         picked_w = [tile([P, S], U32, f"picked_w{i}") for i in range(2)]
-        picked_s = [tile([P, S], U8, f"picked_s{i}") for i in range(2)]
-        w_dealt = [tile([P, PACK, P], I32, f"w_dealt{i}") for i in range(2)]
-        ws_dealt = [tile([P, PACK, P], U8, f"ws_dealt{i}") for i in range(2)]
+        picked_s = [tile([P, S], U8, "picked_s0")]
+        w_dealt = [tile([P, H], I32, f"w_dealt{i}") for i in range(2)]
+        ws_dealt = [tile([P, H], U8, f"ws_dealt{i}") for i in range(2)]
 
         def deal(i):
-            nc.vector.tensor_copy(out=w_dealt[i][:].rearrange("p t m -> p m t"), in_=w_raw[:].rearrange("p (m t) -> p m t", t=PACK))
-            nc.vector.tensor_copy(out=ws_dealt[i][:].rearrange("p t m -> p m t"), in_=ws_raw[:].rearrange("p (m t) -> p m t", t=PACK))
+            for dealt, raw, run in ((w_dealt[i][:], w_raw[i][:], RUN), (ws_dealt[i][:].bitcast(I32), ws_raw[i][:].bitcast(I32), RUN // 4)):
+                nc.vector.tensor_copy(
+                    out=dealt.rearrange("p (t b e) -> p b t e", t=PACK, e=run), in_=raw.rearrange("p (b t e) -> p b t e", t=PACK, e=run)
+                )
+
+        def product(out, lhs_codes, lhs_scales, rhs_codes, rhs_scales):
+            nc.tensor.matmul_mx(
+                out=out,
+                lhsT=lhs_codes.bitcast(FP8X4),
+                lhsT_scale=lhs_scales,
+                rhs=rhs_codes.bitcast(FP8X4),
+                rhs_scale=rhs_scales,
+                start=True,
+                stop=True,
+            )
 
         def project(i):
-            banks = []
+            banks = [bank(PACK * i + t, f"proj{i}{t}") for t in range(PACK)]
             for t in range(PACK):
-                bank = psum.tile([P, S], F32, name=f"proj{i}{t}", tag=f"bank{i}{t}")
-                nc.tensor.matmul_mx(
-                    out=bank[:],
-                    lhsT=w_dealt[i][:, t, :].bitcast(FP8X4),
-                    lhsT_scale=ws_dealt[i][:, t, :],
-                    rhs=picked_w[i][:].bitcast(FP8X4),
-                    rhs_scale=picked_s[i][:],
-                    start=True,
-                    stop=True,
-                )
-                banks.append(bank)
+                cols = slice(t * P, (t + 1) * P)
+                product(banks[t][:], w_dealt[i][:, cols], ws_dealt[i][:, cols], picked_w[i][:], picked_s[i][:])
             return banks
 
-        nc.vector.tensor_copy(picked_s[0][:], xs[:].indirect(offs_t[:]))
         nc.vector.tensor_copy(picked_w[0][:], xw[:].indirect(offs_t[:]))
+        nc.vector.tensor_copy(picked_s[0][:], xs[:].indirect(offs_t[:]))
         deal(0)
-        nc.sync.dma_start(out=w_raw[:], in_=as_words(w2_words))
-        load_scale_rows([nc.sync] * 4, ws_raw, w2_scales)
         a_banks = project(0)
-        nc.vector.tensor_copy(picked_s[1][:], xs[:].indirect(two_t[:]))
         nc.vector.tensor_copy(picked_w[1][:], xw[:].indirect(two_t[:]))
+        picked_s.append(keep.tile([P, V], U8, name="picked_s1", tag="ws_raw0", align_bytes=64))
+        nc.vector.tensor_copy(picked_s[1][:], xs[:].indirect(two_t[:]))
         deal(1)
         b_banks = project(1)
 
@@ -147,60 +173,78 @@ def tile_picked_keylsm_none_po_kernel(
             cols = slice(u * P, (u + 1) * P)
             nc.vector.quantize_mx(out=z_codes[:, cols].bitcast(FP8X4), scales=z_scales[:, cols], in_=z_grouped[:, u * P * PACK : (u + 1) * P * PACK])
 
-        s_banks = []
-        for u in range(PACK):
-            cols = slice(u * P, (u + 1) * P)
-            bank = psum.tile([P, V], F32, name=f"score{u}", tag=f"bank0{u}")
-            nc.tensor.matmul_mx(
-                out=bank[:],
-                lhsT=z_codes[:, cols].bitcast(FP8X4),
-                lhsT_scale=z_scales[:, cols],
-                rhs=z2_codes[:].bitcast(FP8X4),
-                rhs_scale=z2_scales[:],
-                start=True,
-                stop=True,
-            )
-            s_banks.append(bank)
-
         ex = [tile([P, V], F32, f"ex{u}") for u in range(PACK)]
         ex_inv = tile([P, PACK, V], F32, "ex_inv")
         for u in range(PACK):
-            nc.scalar.activation(ex[u][:], s_banks[u][:], ACT.Exp, scale=0.03125)
-        for u in range(PACK):
-            nc.scalar.activation(ex_inv[:, u, :], s_banks[u][:], ACT.Exp, scale=-0.03125)
+            cols = slice(u * P, (u + 1) * P)
+            score = bank(u, f"score{u}")
+            product(score[:], z_codes[:, cols], z_scales[:, cols], z2_codes[:], z2_scales[:])
+            nc.scalar.activation(ex[u][:], score[:], ACT.Exp, scale=0.03125)
+            nc.scalar.activation(ex_inv[:, u, :], score[:], ACT.Exp, scale=-0.03125)
+
+        ratios = [tile([P, PACK, V], F32, f"ratios{k}") for k in range(2)]
+
+        def look_up(u, first, width):
+            for ratio, lists in zip(ratios, (c1_t, c2_t)):
+                nc.vector.tensor_tensor(
+                    ratio[:, u, first : first + width], ex[u][:].indirect(entries(lists, first, width)), ex_inv[:, u, first : first + width], ALU.mult
+                )
+
+        def add_turned(out, u, cols):
+            for k in range(2):
+                nc.tensor.matmul(out, lhsT=ratios[k][:, u, cols], rhs=identity[:], is_transpose=True, start=(k == 0), stop=(k == 1))
 
         out_codes = tile([P, V], U32, "out_codes")
         out_scales = tile([P, V], U8, "out_scales")
         out_rows = out_0.rearrange("(p u) v -> p u v", u=PACK)
-        first = 0
-        for k, width in enumerate(PIECES):
-            cols = slice(first, first + width)
-            one = tile([P, PACK, width], F32, f"one{k}")
-            both = tile([P, PACK, width], F32, f"both{k}")
-            ratio = tile([P, PACK, width], F32, f"ratio{k}")
-            root = tile([P, PACK, width], F32, f"root{k}")
-            share = tile([P, PACK, width], F32, f"share{k}")
-            grouped = tile([P, width * PACK], BF16, f"grouped{k}")
-            last = k == len(PIECES) - 1
-            for step in range(PACK + 2):
-                if step < PACK:
-                    u = step
-                    nc.vector.tensor_copy(one[:, u, :], ex[u][:].indirect(entries(c1_t, first, width)))
-                if 1 <= step <= PACK:
-                    u = step - 1
-                    nc.vector.tensor_tensor(both[:, u, :], ex[u][:].indirect(entries(c2_t, first, width)), one[:, u, :], ALU.add)
-                if last and step >= 2:
-                    u = step - 2
-                    nc.vector.tensor_tensor(ratio[:, u, :], both[:, u, :], ex_inv[:, u, cols], ALU.mult)
-                    nc.scalar.activation(root[:, u, :], ratio[:, u, :], ACT.Abs_reciprocal_sqrt, bias=1.0)
-            if not last:
-                nc.vector.tensor_tensor(ratio[:], both[:], ex_inv[:, :, cols], ALU.mult)
-                nc.scalar.activation(root[:], ratio[:], ACT.Abs_reciprocal_sqrt, bias=1.0)
-            nc.scalar.activation(grouped[:].rearrange("p (c u) -> p c u", u=PACK), root[:].rearrange("p u c -> p c u"), ACT.Square)
-            nc.scalar.activation(share[:], root[:], ACT.Square)
-            nc.vector.quantize_mx(out=out_codes[:, cols].bitcast(FP8X4), scales=out_scales[:, cols], in_=grouped[:])
-            nc.sync.dma_start(out=as_words(out_1)[:, cols], in_=out_codes[:, cols].bitcast(I32))
+        blocks = V // P
+
+        def finish(block):
+            cols = slice(block * P, (block + 1) * P)
+            last = block == blocks - 1
+            root = tile([P, PACK, P], F32, f"root{block}")
+            back = bank(block, f"back{block}")
+            if last:
+                for u in range(PACK):
+                    look_up(u, block * P, P)
+                    total = bank(PACK + (block + u) % PACK, f"total{block}{u}")
+                    add_turned(total[:, :P], u, cols)
+                    nc.scalar.activation(root[:, u, :], total[:, :P], ACT.Abs_reciprocal_sqrt, bias=1.0)
+                    nc.tensor.transpose(back[:, u * P : (u + 1) * P], root[:, u, :], identity[:])
+            else:
+                total = bank(PACK + block, f"total{block}")
+                for u in range(PACK):
+                    add_turned(total[:, u * P : (u + 1) * P], u, cols)
+                nc.scalar.activation(root[:].rearrange("p u m -> p (u m)"), total[:], ACT.Abs_reciprocal_sqrt, bias=1.0)
+                for u in range(PACK):
+                    nc.tensor.transpose(back[:, u * P : (u + 1) * P], root[:, u, :], identity[:])
+            share = tile([P, PACK, P], F32, f"share{block}")
+            grouped = tile([P, P * PACK], BF16, f"grouped{block}")
+            if last:
+                nc.scalar.activation(grouped[:].rearrange("p (c u) -> p c u", u=PACK), back[:].rearrange("p (u c) -> p c u", u=PACK), ACT.Square)
+            nc.scalar.activation(share[:].rearrange("p u c -> p (u c)"), back[:], ACT.Square)
             nc.sync.dma_start(out=out_rows[:, :, cols], in_=share[:])
-            first = first + width
+            return share, grouped
+
+        def hand_on(block, share, grouped):
+            cols = slice(block * P, (block + 1) * P)
+            if block < blocks - 1:
+                nc.vector.tensor_copy(
+                    out=grouped[:].rearrange("p (c i u) -> p c u i", i=PACK, u=PACK), in_=share[:].rearrange("p u (c i) -> p c u i", i=PACK)
+                )
+            nc.vector.quantize_mx(out=out_codes[:, cols].bitcast(FP8X4), scales=out_scales[:, cols], in_=grouped[:])
+
+        for u in range(PACK):
+            look_up(u, 0, HALF)
+        done = [finish(0), finish(1)]
+        for u in range(PACK):
+            look_up(u, HALF, P)
+        done.append(finish(2))
+        done.append(finish(3))
+        for block in range(blocks):
+            hand_on(block, done[block][0], done[block][1])
+        for cols in (slice(0, V - P), slice(V - P, V)):
+            nc.sync.dma_start(out=as_words(out_1)[:, cols], in_=out_codes[:, cols].bitcast(I32))
         for q in range(4):
-            nc.sync.dma_start(out=out_2[0, 4 * q : 4 * q + 4, :].bitcast(I32), in_=out_scales[32 * q : 32 * q + 4, :].bitcast(I32))
+            queue = nc.sync if q < 2 else nc.scalar
+            queue.dma_start(out=out_2[0, 4 * q : 4 * q + 4, :].bitcast(I32), in_=out_scales[32 * q : 32 * q + 4, :].bitcast(I32))

@@ -21,7 +21,8 @@ PACK = 4
 RUN = 8
 LIST_ROWS = 16
 HALF = 256
-PIECES = (256, 128, 128)
+BANKS = 8
+LAG = 2
 
 
 def as_words(dram):
@@ -67,8 +68,8 @@ def tile_picked_keylsm_none_po_kernel(
         nc.vector.memset(ws_raw[0][:].bitcast(I32), 0)
         nc.gpsimd.memset(gain_rows[:], 0.0)
 
-        def load_gain(gain):
-            nc.gpsimd.dma_start(
+        def load_gain(queue, gain):
+            queue.dma_start(
                 out=gain_rows[0:PACK, :].rearrange("t (b e) -> t b e", e=RUN), in_=gain.rearrange("(b t e) o -> t b (e o)", t=PACK, e=RUN)
             )
 
@@ -80,7 +81,7 @@ def tile_picked_keylsm_none_po_kernel(
         nc.sync.dma_start(out=xw[:].bitcast(I32), in_=as_words(x_words))
         load_scale_rows(nc.sync, xs, x_scales)
         load_scale_rows(nc.sync, ws_raw[0], w1_scales)
-        load_gain(ga)
+        load_gain(nc.gpsimd, ga)
         make_identity(nc, identity[:])
         nc.gpsimd.dma_start(out=w_raw[0][:], in_=as_words(w1_words))
         nc.gpsimd.memset(ws_raw[1][:].bitcast(I32), 0)
@@ -94,15 +95,18 @@ def tile_picked_keylsm_none_po_kernel(
         nc.tensor.transpose(turned[:, :P], gain_rows[:], identity[:])
         nc.scalar.activation(half_ga[:], turned[:, :PACK], ACT.Copy, scale=0.5)
         nc.scalar.copy(ga_t[:], turned[:, :PACK])
-        load_gain(gb)
+        load_gain(nc.sync, gb)
         turned = bank(7, "gb_turned")
         nc.tensor.transpose(turned[:, :P], gain_rows[:], identity[:])
         nc.scalar.copy(gb_t[:], turned[:, :PACK])
 
-        picked_w = [tile([P, S], U32, f"picked_w{i}") for i in range(2)]
+        picked_w = [tile([P, S], U32, "picked_w0")]
         picked_s = [tile([P, S], U8, "picked_s0")]
-        w_dealt = [tile([P, H], I32, f"w_dealt{i}") for i in range(2)]
-        ws_dealt = [tile([P, H], U8, f"ws_dealt{i}") for i in range(2)]
+        w_dealt = [tile([P, H], I32, "w_dealt0")]
+        ws_dealt = [tile([P, H], U8, "ws_dealt0")]
+
+        def reuse(dtype, name, tag):
+            return keep.tile([P, 512], dtype, name=name, tag=tag, align_bytes=64)
 
         def deal(i):
             for dealt, raw, run in ((w_dealt[i][:], w_raw[i][:], RUN), (ws_dealt[i][:].bitcast(I32), ws_raw[i][:].bitcast(I32), RUN // 4)):
@@ -132,9 +136,12 @@ def tile_picked_keylsm_none_po_kernel(
         nc.vector.tensor_copy(picked_s[0][:], xs[:].indirect(offs_t[:]))
         deal(0)
         a_banks = project(0)
+        picked_w.append(reuse(U32, "picked_w1", "w_raw0"))
+        picked_s.append(reuse(U8, "picked_s1", "ws_raw0"))
         nc.vector.tensor_copy(picked_w[1][:], xw[:].indirect(two_t[:]))
-        picked_s.append(keep.tile([P, V], U8, name="picked_s1", tag="ws_raw0", align_bytes=64))
         nc.vector.tensor_copy(picked_s[1][:], xs[:].indirect(two_t[:]))
+        w_dealt.append(reuse(I32, "w_dealt1", "picked_w0"))
+        ws_dealt.append(reuse(U8, "ws_dealt1", "picked_s0"))
         deal(1)
         b_banks = project(1)
 
@@ -155,20 +162,18 @@ def tile_picked_keylsm_none_po_kernel(
         nc.vector.tensor_copy(
             out=z_grouped[:].rearrange("p (u m t) -> p m t u", u=PACK, t=PACK), in_=z[:].rearrange("p t (m u) -> p m t u", u=PACK)
         )
-        z2_grouped = [tile([P, HALF * PACK], BF16, f"z2_grouped{h}") for h in range(2)]
-        for h, copy in enumerate((nc.vector.tensor_copy, nc.scalar.copy)):
+        z2_grouped = tile([P, V, PACK], BF16, "z2_grouped")
+        for cols, copy in ((slice(0, P), nc.vector.tensor_copy), (slice(P, V), nc.scalar.copy)):
             copy(
-                out=z2_grouped[h][:].rearrange("p (c i t) -> p c t i", i=PACK, t=PACK),
-                in_=z2[:, :, h * HALF : (h + 1) * HALF].rearrange("p t (c i) -> p c t i", i=PACK),
+                out=z2_grouped[:, cols, :].rearrange("p (c i) t -> p c t i", i=PACK),
+                in_=z2[:, :, cols].rearrange("p t (c i) -> p c t i", i=PACK),
             )
         z_codes = tile([P, S], U32, "z_codes")
         z_scales = tile([P, S], U8, "z_scales")
         z2_codes = tile([P, V], U32, "z2_codes")
         z2_scales = tile([P, V], U8, "z2_scales")
         nc.vector.quantize_mx(out=z_codes[:, :P].bitcast(FP8X4), scales=z_scales[:, :P], in_=z_grouped[:, : P * PACK])
-        for h in range(2):
-            cols = slice(h * HALF, (h + 1) * HALF)
-            nc.vector.quantize_mx(out=z2_codes[:, cols].bitcast(FP8X4), scales=z2_scales[:, cols], in_=z2_grouped[h][:])
+        nc.vector.quantize_mx(out=z2_codes[:].bitcast(FP8X4), scales=z2_scales[:], in_=z2_grouped[:].rearrange("p c t -> p (c t)"))
         for u in range(1, PACK):
             cols = slice(u * P, (u + 1) * P)
             nc.vector.quantize_mx(out=z_codes[:, cols].bitcast(FP8X4), scales=z_scales[:, cols], in_=z_grouped[:, u * P * PACK : (u + 1) * P * PACK])
@@ -180,70 +185,54 @@ def tile_picked_keylsm_none_po_kernel(
             score = bank(u, f"score{u}")
             product(score[:], z_codes[:, cols], z_scales[:, cols], z2_codes[:], z2_scales[:])
             nc.scalar.activation(ex[u][:], score[:], ACT.Exp, scale=0.03125)
-            nc.scalar.activation(ex_inv[:, u, :], score[:], ACT.Exp, scale=-0.03125)
-
-        ratios = [tile([P, PACK, V], F32, f"ratios{k}") for k in range(2)]
-
-        def look_up(u, first, width):
-            for ratio, lists in zip(ratios, (c1_t, c2_t)):
-                nc.vector.tensor_tensor(
-                    ratio[:, u, first : first + width], ex[u][:].indirect(entries(lists, first, width)), ex_inv[:, u, first : first + width], ALU.mult
-                )
-
-        def add_turned(out, u, cols):
-            for k in range(2):
-                nc.tensor.matmul(out, lhsT=ratios[k][:, u, cols], rhs=identity[:], is_transpose=True, start=(k == 0), stop=(k == 1))
+            for j in range(0, V, HALF):
+                nc.scalar.activation(ex_inv[:, u, j : j + HALF], score[:, j : j + HALF], ACT.Exp, scale=-0.03125)
 
         out_codes = tile([P, V], U32, "out_codes")
         out_scales = tile([P, V], U8, "out_scales")
+        share = tile([P, PACK, V], F32, "share")
         out_rows = out_0.rearrange("(p u) v -> p u v", u=PACK)
-        blocks = V // P
+        last = PACK - 1
+        pieces = [slice(0, HALF), slice(HALF, V - P), slice(V - P, V)]
+        steps = [(u, slice(0, V)) for u in range(last)] + [(last, cols) for cols in pieces]
 
-        def finish(block):
-            cols = slice(block * P, (block + 1) * P)
-            last = block == blocks - 1
-            root = tile([P, PACK, P], F32, f"root{block}")
-            back = bank(block, f"back{block}")
-            if last:
-                for u in range(PACK):
-                    look_up(u, block * P, P)
-                    total = bank(PACK + (block + u) % PACK, f"total{block}{u}")
-                    add_turned(total[:, :P], u, cols)
-                    nc.scalar.activation(root[:, u, :], total[:, :P], ACT.Abs_reciprocal_sqrt, bias=1.0)
-                    nc.tensor.transpose(back[:, u * P : (u + 1) * P], root[:, u, :], identity[:])
+        for step, (u, cols) in enumerate(steps):
+            width = cols.stop - cols.start
+            ratios = [tile([P, width], F32, f"ratio{step}{k}") for k in range(2)]
+            for j in range(0, width, HALF):
+                count = min(HALF, width)
+                for ratio, lists in zip(ratios, (c1_t, c2_t)):
+                    at = cols.start + j
+                    nc.vector.tensor_tensor(
+                        ratio[:, j : j + count], ex[u][:].indirect(entries(lists, at, count)), ex_inv[:, u, at : at + count], ALU.mult
+                    )
+            root = keep.tile([P, width], F32, name=f"root{step}", tag=f"root{min(step, len(steps) - 2)}", align_bytes=64)
+            if step == len(steps) - 1:
+                summed = tile([P, width], F32, "summed")
+                nc.vector.tensor_tensor(summed[:], ratios[0][:], ratios[1][:], ALU.add)
+                nc.scalar.activation(root[:], summed[:], ACT.Abs_reciprocal_sqrt, bias=1.0)
+                nc.scalar.activation(share[:, u, cols], root[:], ACT.Square)
             else:
-                total = bank(PACK + block, f"total{block}")
-                for u in range(PACK):
-                    add_turned(total[:, u * P : (u + 1) * P], u, cols)
-                nc.scalar.activation(root[:].rearrange("p u m -> p (u m)"), total[:], ACT.Abs_reciprocal_sqrt, bias=1.0)
-                for u in range(PACK):
-                    nc.tensor.transpose(back[:, u * P : (u + 1) * P], root[:, u, :], identity[:])
-            share = tile([P, PACK, P], F32, f"share{block}")
-            grouped = tile([P, P * PACK], BF16, f"grouped{block}")
-            if last:
-                nc.scalar.activation(grouped[:].rearrange("p (c u) -> p c u", u=PACK), back[:].rearrange("p (u c) -> p c u", u=PACK), ACT.Square)
-            nc.scalar.activation(share[:].rearrange("p u c -> p (u c)"), back[:], ACT.Square)
-            nc.sync.dma_start(out=out_rows[:, :, cols], in_=share[:])
-            return share, grouped
+                total = bank((step - LAG) % BANKS, f"total{step}")
+                for j in range(0, width, P):
+                    for k in range(2):
+                        nc.tensor.matmul(
+                            total[:, j : j + P], lhsT=ratios[k][:, j : j + P], rhs=identity[:], is_transpose=True, start=(k == 0), stop=(k == 1)
+                        )
+                nc.scalar.activation(root[:], total[:, :width], ACT.Abs_reciprocal_sqrt, bias=1.0)
+                back = bank(step, f"back{step}")
+                for j in range(0, width, P):
+                    nc.tensor.transpose(back[:, j : j + P], root[:, j : j + P], identity[:])
+                nc.scalar.activation(share[:, u, cols], back[:, :width], ACT.Square)
+            nc.sync.dma_start(out=out_rows[:, u, cols], in_=share[:, u, cols])
 
-        def hand_on(block, share, grouped):
-            cols = slice(block * P, (block + 1) * P)
-            if block < blocks - 1:
-                nc.vector.tensor_copy(
-                    out=grouped[:].rearrange("p (c i u) -> p c u i", i=PACK, u=PACK), in_=share[:].rearrange("p u (c i) -> p c u i", i=PACK)
-                )
+        for k, cols in enumerate(pieces):
+            width = cols.stop - cols.start
+            grouped = tile([P, width * PACK], BF16, f"grouped{k}")
+            nc.vector.tensor_copy(
+                out=grouped[:].rearrange("p (c i u) -> p c u i", i=PACK, u=PACK), in_=share[:, :, cols].rearrange("p u (c i) -> p c u i", i=PACK)
+            )
             nc.vector.quantize_mx(out=out_codes[:, cols].bitcast(FP8X4), scales=out_scales[:, cols], in_=grouped[:])
-
-        for u in range(PACK):
-            look_up(u, 0, HALF)
-        done = [finish(0), finish(1)]
-        for u in range(PACK):
-            look_up(u, HALF, P)
-        done.append(finish(2))
-        done.append(finish(3))
-        for block in range(blocks):
-            hand_on(block, done[block][0], done[block][1])
-        for cols in (slice(0, V - P), slice(V - P, V)):
             nc.sync.dma_start(out=as_words(out_1)[:, cols], in_=out_codes[:, cols].bitcast(I32))
         for q in range(4):
             queue = nc.sync if q < 2 else nc.scalar

@@ -158,12 +158,22 @@ def tile_picked_keylsm_none_po_kernel(
         for t in range(PACK):
             nc.scalar.activation(z2[:, t, :], b_banks[t][:], ACT.Copy, scale=gb_t[:, t : t + 1])
 
-        z_grouped = tile([P, S * PACK], BF16, "z_grouped")
-        nc.vector.tensor_copy(
-            out=z_grouped[:].rearrange("p (u m t) -> p m t u", u=PACK, t=PACK), in_=z[:].rearrange("p t (m u) -> p m t u", u=PACK)
-        )
+        z_grouped = [tile([P, 2 * P * PACK], BF16, "z_grouped0")]
+
+        def group_z(h):
+            nc.vector.tensor_copy(
+                out=z_grouped[h][:].rearrange("p (u m t) -> p m t u", u=2, t=PACK),
+                in_=z[:].rearrange("p t (m u) -> p m t u", u=PACK)[:, :, :, 2 * h : 2 * h + 2],
+            )
+
+        def quantize_z(u):
+            cols = slice(u * P, (u + 1) * P)
+            source = z_grouped[u // 2][:, (u % 2) * P * PACK : (u % 2 + 1) * P * PACK]
+            nc.vector.quantize_mx(out=z_codes[:, cols].bitcast(FP8X4), scales=z_scales[:, cols], in_=source)
+
+        group_z(0)
         z2_grouped = tile([P, V, PACK], BF16, "z2_grouped")
-        for cols, copy in ((slice(0, P), nc.vector.tensor_copy), (slice(P, V), nc.scalar.copy)):
+        for cols, copy in ((slice(0, HALF), nc.vector.tensor_copy), (slice(HALF, V), nc.scalar.copy)):
             copy(
                 out=z2_grouped[:, cols, :].rearrange("p (c i) t -> p c t i", i=PACK),
                 in_=z2[:, :, cols].rearrange("p t (c i) -> p c t i", i=PACK),
@@ -172,11 +182,13 @@ def tile_picked_keylsm_none_po_kernel(
         z_scales = tile([P, S], U8, "z_scales")
         z2_codes = tile([P, V], U32, "z2_codes")
         z2_scales = tile([P, V], U8, "z2_scales")
-        nc.vector.quantize_mx(out=z_codes[:, :P].bitcast(FP8X4), scales=z_scales[:, :P], in_=z_grouped[:, : P * PACK])
+        quantize_z(0)
         nc.vector.quantize_mx(out=z2_codes[:].bitcast(FP8X4), scales=z2_scales[:], in_=z2_grouped[:].rearrange("p c t -> p (c t)"))
-        for u in range(1, PACK):
-            cols = slice(u * P, (u + 1) * P)
-            nc.vector.quantize_mx(out=z_codes[:, cols].bitcast(FP8X4), scales=z_scales[:, cols], in_=z_grouped[:, u * P * PACK : (u + 1) * P * PACK])
+        quantize_z(1)
+        z_grouped.append(keep.tile([P, 2 * P * PACK], BF16, name="z_grouped1", tag="z2_grouped", align_bytes=64))
+        group_z(1)
+        quantize_z(2)
+        quantize_z(3)
 
         ex = [tile([P, V], F32, f"ex{u}") for u in range(PACK)]
         ex_inv = tile([P, PACK, V], F32, "ex_inv")

from contextlib import ExitStack

import concourse.mybir as mybir
from concourse.masks import make_identity

K, T, S, V, H = 512, 2048, 512, 512, 512
FLOPS = 3 * 2 * 512 * 512 * 512

F32 = mybir.dt.float32
BF16 = mybir.dt.bfloat16
I32 = mybir.dt.int32
U32 = mybir.dt.uint32
U16 = mybir.dt.uint16
U8 = mybir.dt.uint8
FP8X4 = mybir.dt.float8_e4m3fn_x4
ACT = mybir.ActivationFunctionType
ALU = mybir.AluOpType

P = 128
PACK = 4
RUN = 8
LIST_ROWS = 16
HALF = 256
BANKS = 8
LAG = 2


def as_words(dram):
    return dram[0].rearrange("p n t -> p (n t)").bitcast(I32)


def entries(lists, first, count):
    return lists[:, first // LIST_ROWS : (first + count) // LIST_ROWS]


def load_scale_rows(queue, plane, rows):
    for q in range(4):
        queue.dma_start(out=plane[32 * q : 32 * q + 4, :].bitcast(I32), in_=rows[0, 4 * q : 4 * q + 4, :].bitcast(I32))


def tile_picked_keylsm_none_po_kernel(
    tc, x_words, x_scales, w1_words, w1_scales, w2_words, w2_scales, ga, gb, offs, two, n1, c1, c2, out_0, out_1, out_2
):
    nc = tc.nc
    with ExitStack() as ctx:
        keep = ctx.enter_context(tc.tile_pool(name="keep", bufs=1))
        psum = ctx.enter_context(tc.psum_pool(name="psum", bufs=1))

        def tile(shape, dtype, name):
            return keep.tile(shape, dtype, name=name, align_bytes=64)

        def bank(index, name):
            return psum.tile([P, 512], F32, name=name, tag=f"bank{index}")

        offs_t = tile([P, S // LIST_ROWS], U16, "offs_t")
        two_t = tile([P, V // LIST_ROWS], U16, "two_t")
        n1_t = tile([P, S // LIST_ROWS], U16, "n1_t")
        c1_t = tile([P, V // LIST_ROWS], U16, "c1_t")
        c2_t = tile([P, V // LIST_ROWS], U16, "c2_t")
        xw = tile([P, T], U32, "xw")
        xs = tile([P, T], U8, "xs")
        w_raw = [tile([P, H], I32, f"w_raw{i}") for i in range(2)]
        ws_raw = [tile([P, H], U8, f"ws_raw{i}") for i in range(2)]
        gain_rows = tile([P, P], F32, "gain_rows")
        identity = tile([P, P], F32, "identity")

        nc.vector.memset(xs[:].bitcast(I32), 0)
        nc.vector.memset(ws_raw[0][:].bitcast(I32), 0)
        nc.gpsimd.memset(gain_rows[:], 0.0)

        def load_gain(queue, gain):
            queue.dma_start(
                out=gain_rows[0:PACK, :].rearrange("t (b e) -> t b e", e=RUN), in_=gain.rearrange("(b t e) o -> t b (e o)", t=PACK, e=RUN)
            )

        nc.sync.dma_start(offs_t[:], offs)
        nc.sync.dma_start(two_t[:], two)
        nc.sync.dma_start(n1_t[:], n1)
        nc.sync.dma_start(c1_t[:], c1)
        nc.sync.dma_start(c2_t[:], c2)
        nc.sync.dma_start(out=xw[:].bitcast(I32), in_=as_words(x_words))
        load_scale_rows(nc.sync, xs, x_scales)
        load_scale_rows(nc.sync, ws_raw[0], w1_scales)
        load_gain(nc.gpsimd, ga)
        make_identity(nc, identity[:])
        nc.gpsimd.dma_start(out=w_raw[0][:], in_=as_words(w1_words))
        nc.gpsimd.memset(ws_raw[1][:].bitcast(I32), 0)
        nc.gpsimd.dma_start(out=w_raw[1][:], in_=as_words(w2_words))
        load_scale_rows(nc.sync, ws_raw[1], w2_scales)

        ga_t = tile([P, PACK], F32, "ga_t")
        half_ga = tile([P, PACK], F32, "half_ga")
        gb_t = tile([P, PACK], F32, "gb_t")
        turned = bank(6, "ga_turned")
        nc.tensor.transpose(turned[:, :P], gain_rows[:], identity[:])
        nc.scalar.activation(half_ga[:], turned[:, :PACK], ACT.Copy, scale=0.5)
        nc.scalar.copy(ga_t[:], turned[:, :PACK])
        load_gain(nc.sync, gb)
        turned = bank(7, "gb_turned")
        nc.tensor.transpose(turned[:, :P], gain_rows[:], identity[:])
        nc.scalar.copy(gb_t[:], turned[:, :PACK])

        picked_w = [tile([P, S], U32, "picked_w0")]
        picked_s = [tile([P, S], U8, "picked_s0")]
        w_dealt = [tile([P, H], I32, "w_dealt0")]
        ws_dealt = [tile([P, H], U8, "ws_dealt0")]

        def reuse(dtype, name, tag):
            return keep.tile([P, 512], dtype, name=name, tag=tag, align_bytes=64)

        def deal(i):
            for dealt, raw, run in ((w_dealt[i][:], w_raw[i][:], RUN), (ws_dealt[i][:].bitcast(I32), ws_raw[i][:].bitcast(I32), RUN // 4)):
                nc.vector.tensor_copy(
                    out=dealt.rearrange("p (t b e) -> p b t e", t=PACK, e=run), in_=raw.rearrange("p (b t e) -> p b t e", t=PACK, e=run)
                )

        def product(out, lhs_codes, lhs_scales, rhs_codes, rhs_scales):
            nc.tensor.matmul_mx(
                out=out,
                lhsT=lhs_codes.bitcast(FP8X4),
                lhsT_scale=lhs_scales,
                rhs=rhs_codes.bitcast(FP8X4),
                rhs_scale=rhs_scales,
                start=True,
                stop=True,
            )

        def project(i):
            banks = [bank(PACK * i + t, f"proj{i}{t}") for t in range(PACK)]
            for t in range(PACK):
                cols = slice(t * P, (t + 1) * P)
                product(banks[t][:], w_dealt[i][:, cols], ws_dealt[i][:, cols], picked_w[i][:], picked_s[i][:])
            return banks

        nc.vector.tensor_copy(picked_w[0][:], xw[:].indirect(offs_t[:]))
        nc.vector.tensor_copy(picked_s[0][:], xs[:].indirect(offs_t[:]))
        deal(0)
        a_banks = project(0)
        picked_w.append(reuse(U32, "picked_w1", "w_raw0"))
        picked_s.append(reuse(U8, "picked_s1", "ws_raw0"))
        nc.vector.tensor_copy(picked_w[1][:], xw[:].indirect(two_t[:]))
        nc.vector.tensor_copy(picked_s[1][:], xs[:].indirect(two_t[:]))
        w_dealt.append(reuse(I32, "w_dealt1", "picked_w0"))
        ws_dealt.append(reuse(U8, "ws_dealt1", "picked_s0"))
        deal(1)
        b_banks = project(1)

        z = tile([P, PACK, S], F32, "z")
        a_full = tile([P, PACK, S], F32, "a_full")
        for t in range(PACK):
            a_half = tile([P, S], F32, f"a_half{t}")
            nc.scalar.activation(a_half[:], a_banks[t][:], ACT.Copy, scale=half_ga[:, t : t + 1])
            nc.scalar.activation(a_full[:, t, :], a_banks[t][:], ACT.Copy, scale=ga_t[:, t : t + 1])
            for j in range(0, S, HALF):
                nc.vector.tensor_tensor(z[:, t, j : j + HALF], a_half[:].indirect(entries(n1_t, j, HALF)), a_full[:, t, j : j + HALF], ALU.add)

        z2 = tile([P, PACK, V], BF16, "z2")
        for t in range(PACK):
            nc.scalar.activation(z2[:, t, :], b_banks[t][:], ACT.Copy, scale=gb_t[:, t : t + 1])

        z_grouped = [tile([P, 2 * P * PACK], BF16, "z_grouped0")]

        def group_z(h):
            nc.vector.tensor_copy(
                out=z_grouped[h][:].rearrange("p (u m t) -> p m t u", u=2, t=PACK),
                in_=z[:].rearrange("p t (m u) -> p m t u", u=PACK)[:, :, :, 2 * h : 2 * h + 2],
            )

        def quantize_z(u):
            cols = slice(u * P, (u + 1) * P)
            source = z_grouped[u // 2][:, (u % 2) * P * PACK : (u % 2 + 1) * P * PACK]
            nc.vector.quantize_mx(out=z_codes[:, cols].bitcast(FP8X4), scales=z_scales[:, cols], in_=source)

        group_z(0)
        z2_grouped = tile([P, V, PACK], BF16, "z2_grouped")
        for cols, copy in ((slice(0, HALF), nc.vector.tensor_copy), (slice(HALF, V), nc.scalar.copy)):
            copy(
                out=z2_grouped[:, cols, :].rearrange("p (c i) t -> p c t i", i=PACK),
                in_=z2[:, :, cols].rearrange("p t (c i) -> p c t i", i=PACK),
            )
        z_codes = tile([P, S], U32, "z_codes")
        z_scales = tile([P, S], U8, "z_scales")
        z2_codes = tile([P, V], U32, "z2_codes")
        z2_scales = tile([P, V], U8, "z2_scales")
        quantize_z(0)
        nc.vector.quantize_mx(out=z2_codes[:].bitcast(FP8X4), scales=z2_scales[:], in_=z2_grouped[:].rearrange("p c t -> p (c t)"))
        quantize_z(1)
        z_grouped.append(keep.tile([P, 2 * P * PACK], BF16, name="z_grouped1", tag="z2_grouped", align_bytes=64))
        group_z(1)
        quantize_z(2)
        quantize_z(3)

        ex = [tile([P, V], F32, f"ex{u}") for u in range(PACK)]
        ex_inv = tile([P, PACK, V], F32, "ex_inv")
        for u in range(PACK):
            cols = slice(u * P, (u + 1) * P)
            score = bank(u, f"score{u}")
            product(score[:], z_codes[:, cols], z_scales[:, cols], z2_codes[:], z2_scales[:])
            nc.scalar.activation(ex[u][:], score[:], ACT.Exp, scale=0.03125)
            for j in range(0, V, HALF):
                nc.scalar.activation(ex_inv[:, u, j : j + HALF], score[:, j : j + HALF], ACT.Exp, scale=-0.03125)

        out_codes = tile([P, V], U32, "out_codes")
        out_scales = tile([P, V], U8, "out_scales")
        share = tile([P, PACK, V], F32, "share")
        out_rows = out_0.rearrange("(p u) v -> p u v", u=PACK)
        last = PACK - 1
        pieces = [slice(0, HALF), slice(HALF, V - P), slice(V - P, V)]
        steps = [(u, slice(0, V)) for u in range(last)] + [(last, cols) for cols in pieces]

        for step, (u, cols) in enumerate(steps):
            width = cols.stop - cols.start
            ratios = [tile([P, width], F32, f"ratio{step}{k}") for k in range(2)]
            for j in range(0, width, HALF):
                count = min(HALF, width)
                for ratio, lists in zip(ratios, (c1_t, c2_t)):
                    at = cols.start + j
                    nc.vector.tensor_tensor(
                        ratio[:, j : j + count], ex[u][:].indirect(entries(lists, at, count)), ex_inv[:, u, at : at + count], ALU.mult
                    )
            root = keep.tile([P, width], F32, name=f"root{step}", tag=f"root{min(step, len(steps) - 2)}", align_bytes=64)
            if step == len(steps) - 1:
                summed = tile([P, width], F32, "summed")
                nc.vector.tensor_tensor(summed[:], ratios[0][:], ratios[1][:], ALU.add)
                nc.scalar.activation(root[:], summed[:], ACT.Abs_reciprocal_sqrt, bias=1.0)
                nc.scalar.activation(share[:, u, cols], root[:], ACT.Square)
            else:
                total = bank((step - LAG) % BANKS, f"total{step}")
                for j in range(0, width, P):
                    for k in range(2):
                        nc.tensor.matmul(
                            total[:, j : j + P], lhsT=ratios[k][:, j : j + P], rhs=identity[:], is_transpose=True, start=(k == 0), stop=(k == 1)
                        )
                nc.scalar.activation(root[:], total[:, :width], ACT.Abs_reciprocal_sqrt, bias=1.0)
                back = bank(step, f"back{step}")
                for j in range(0, width, P):
                    nc.tensor.transpose(back[:, j : j + P], root[:, j : j + P], identity[:])
                nc.scalar.activation(share[:, u, cols], back[:, :width], ACT.Square)
            nc.sync.dma_start(out=out_rows[:, u, cols], in_=share[:, u, cols])

        for k, cols in enumerate(pieces):
            width = cols.stop - cols.start
            grouped = tile([P, width * PACK], BF16, f"grouped{k}")
            nc.vector.tensor_copy(
                out=grouped[:].rearrange("p (c i u) -> p c u i", i=PACK, u=PACK), in_=share[:, :, cols].rearrange("p u (c i) -> p c u i", i=PACK)
            )
            nc.vector.quantize_mx(out=out_codes[:, cols].bitcast(FP8X4), scales=out_scales[:, cols], in_=grouped[:])
            nc.sync.dma_start(out=as_words(out_1)[:, cols], in_=out_codes[:, cols].bitcast(I32))
        for q in range(4):
            queue = nc.sync if q < 2 else nc.scalar
            queue.dma_start(out=out_2[0, 4 * q : 4 * q + 4, :].bitcast(I32), in_=out_scales[32 * q : 32 * q + 4, :].bitcast(I32))
